import numpy as np
import ml_dtypes


def mxq(x, axis, fmt="e4m3"):
    dtype, down = {"e4m3": (ml_dtypes.float8_e4m3fn, 7), "e5m2": (ml_dtypes.float8_e5m2, 14)}[fmt]
    v = np.moveaxis(np.asarray(x, np.float32).astype(ml_dtypes.bfloat16).astype(np.float64), axis, -1)
    blocks = v.reshape(v.shape[:-1] + (-1, 32))
    amax = np.abs(blocks).max(-1, keepdims=True)
    byte = np.maximum(np.where(amax > 0, np.frexp(amax)[1] - 1 + 127, 0) - down, 1)
    scale = np.exp2(byte - 127.0)
    codes = (blocks / scale).astype(np.float32).astype(dtype).astype(np.float64)
    return np.moveaxis((codes * scale).reshape(v.shape), -1, axis)


WIDE = False


def mx_kscale(k):
    if not WIDE:
        return np.ones(k)
    levels = np.array([10, -10, 5, -5, 0])
    if k % 512:
        return np.exp2(np.random.permutation(np.resize(levels, k // 32))).repeat(32)
    a = np.empty((k // 512, 16))
    for p in range(k // 512):
        a[p, :8] = np.random.permutation(np.resize(levels, 8))
        for g in range(8):
            far = levels[np.abs(levels - a[p, g]) >= 10]
            a[p, g + 8] = far[np.random.randint(len(far))]
    return np.exp2(a.ravel()).repeat(32)


def f64(x):
    return np.asarray(x).astype(np.float64)


def striped(idx):
    return np.tile(idx.reshape(-1, 16).T, (8, 1)).astype(np.uint16)


def unstriped(offs):
    return offs[:16].T.reshape(-1).astype(np.int64)


def pack_weight(w):
    k, n = w.shape
    w = f64(np.asarray(w, np.float32).astype(ml_dtypes.bfloat16)).reshape(k // 32, 32, n)
    amax = np.abs(w).max(1)
    byte = np.clip(np.where(amax > 0, np.frexp(amax)[1] - 1 + 127 - 7, 1), 1, 254)
    scaled = (w * np.exp2(127.0 - byte)[:, None, :]).reshape(k, n).astype(np.float32)
    words = np.ascontiguousarray(scaled.reshape(k // 512, 128, 4, n).transpose(0, 1, 3, 2)).astype(ml_dtypes.float8_e4m3fn).view(np.uint8)
    return words, np.ascontiguousarray(byte.astype(np.uint8).reshape(k // 512, 16, n))


def unpack_weight(words, scales):
    g, p, n, _ = words.shape
    vals = np.ascontiguousarray(words).view(ml_dtypes.float8_e4m3fn).astype(np.float64) * np.repeat(np.exp2(scales.astype(np.float64) - 127.0), 8, axis=1)[..., None]
    return vals.transpose(0, 1, 3, 2).reshape(g * 512, n)


E2M1 = np.array([0.0, 0.5, 1.0, 1.5, 2.0, 3.0, 4.0, 6.0, -0.0, -0.5, -1.0, -1.5, -2.0, -3.0, -4.0, -6.0])


def pack_fp4(w):
    k, n = w.shape
    w = f64(np.asarray(w, np.float32).astype(ml_dtypes.bfloat16)).reshape(k // 32, 32, n)
    amax = np.abs(w).max(1)
    mant, ex = np.frexp(amax / 6.0)
    byte = np.clip(np.where(amax > 0, np.where(mant > 0.5, ex, ex - 1) + 127, 1), 1, 254)
    scaled = (w * np.exp2(127.0 - byte)[:, None, :]).reshape(k, n).astype(np.float32)
    c = np.ascontiguousarray(scaled.reshape(k // 512, 128, 4, n).transpose(0, 1, 3, 2)).astype(ml_dtypes.float4_e2m1fn).view(np.uint8) & 0xF
    words = (c[..., 0::2] | (c[..., 1::2] << 4)).reshape(k // 512, 128, 2 * n)
    return np.ascontiguousarray(words), np.ascontiguousarray(byte.astype(np.uint8).reshape(k // 512, 16, n))


def unpack_fp4(words, scales):
    g, _, n = scales.shape
    words = np.ascontiguousarray(words).reshape(g, 128, n, 2)
    nib = np.empty((g, 128, n, 4), np.uint8)
    nib[..., 0::2] = words & 0xF
    nib[..., 1::2] = words >> 4
    vals = E2M1[nib] * np.repeat(np.exp2(scales.astype(np.float64) - 127.0), 8, axis=1)[..., None]
    return vals.transpose(0, 1, 3, 2).reshape(g * 512, n)


K, T, S, D, N, H, V, U = 1024, 2048, 1024, 4, 128, 512, 256, 512


def setup_inputs():
    n = np.random.standard_normal
    s = mx_kscale(K)[:, None]
    u = mx_kscale(H)
    packed_xT = pack_weight(n((K, T)) * s)
    packed_w1 = pack_fp4(n((K, H)) / np.sqrt(K) / s)
    packed_w2 = pack_fp4(n((H, N)) / np.sqrt(H) / u[:, None])
    return {
        "x_words": packed_xT[0],
        "x_scales": packed_xT[1],
        "w1_words": packed_w1[0],
        "w1_scales": packed_w1[1],
        "lw": (np.random.uniform(0.5, 1.5, (H, U))).astype(np.float32),
        "unit": (np.random.uniform(0.6, 1.4, (H, 1)) * u[:, None]).astype(np.float32),
        "w2_words": packed_w2[0],
        "w2_scales": packed_w2[1],
        "offs": striped(np.random.permutation(T)[:S]),
        "shf": striped(np.random.permutation(S)),
        "lag": striped(np.random.permutation(np.concatenate([np.arange(V), np.random.randint(0, V, U - V)]))),
    }


def reference(x_words, x_scales, w1_words, w1_scales, lw, unit, w2_words, w2_scales, offs, shf, lag):
    xq = unpack_weight(x_words, x_scales)[:, unstriped(offs)]
    y = unpack_fp4(w1_words, w1_scales).T @ xq
    ys = y[:, unstriped(shf)]
    dif = y - ys
    rootd = np.sqrt(np.abs(dif) + 0.05)
    rmean = rootd.reshape(len(rootd), -1, D).mean(axis=2)
    cress = (((rmean) ** 2) ** 2) / (0.5 * ((rmean) ** 2) + 0.6)
    cl = cress[:, unstriped(lag)]
    cw = cl * f64(lw)
    hid = f64(unit) * (np.log(cw + 0.2) + rmean[:, unstriped(lag)])
    return unpack_fp4(w2_words, w2_scales).T @ mxq(hid, 0, "e4m3")

@@ -1,0 +1,233 @@
+from contextlib import ExitStack
+
+import concourse.mybir as mybir
+
+K, T, S, D, N, H, V, U = 1024, 2048, 1024, 4, 128, 512, 256, 512
+FLOPS = 2 * K * H * S + 2 * H * N * U
+
+F32 = mybir.dt.float32
+BF16 = mybir.dt.bfloat16
+I32 = mybir.dt.int32
+U32 = mybir.dt.uint32
+U16 = mybir.dt.uint16
+U8 = mybir.dt.uint8
+FP8X4 = mybir.dt.float8_e4m3fn_x4
+FP4X4 = mybir.dt.float4_e2m1fn_x4
+ALU = mybir.AluOpType
+ACT = mybir.ActivationFunctionType
+
+P = 128
+PACK = 4
+PASSES = K // (P * PACK)
+QUADS = 4
+HALF = S // 2
+RHALF = U // 2
+LIST_ROWS = 16
+
+
+def tile_picked_yvario_log_p_kernel(
+    tc, x_words, x_scales, w1_words, w1_scales, lw, unit, w2_words, w2_scales, offs, shf, lag, out
+):
+    nc = tc.nc
+    with ExitStack() as ctx:
+        keep = ctx.enter_context(tc.tile_pool(name="keep", bufs=1))
+        psum = ctx.enter_context(tc.psum_pool(name="psum", bufs=1))
+
+        def sb(name, shape, dtype):
+            return keep.tile(shape, dtype, name=name, align_bytes=64)
+
+        def entries(list_tile, first, count):
+            return list_tile[:, first // LIST_ROWS : (first + count) // LIST_ROWS]
+
+        offs_sb = sb("offs_sb", [P, S // LIST_ROWS], U16)
+        shf_sb = sb("shf_sb", [P, S // LIST_ROWS], U16)
+        lag_sb = sb("lag_sb", [P, U // LIST_ROWS], U16)
+        xs_table = sb("xs_table", [P, T], U8)
+        xw_table = [keep.tile([P, T], I32, name=f"xw_table{o}", tag=f"wide{o}", align_bytes=64) for o in range(PASSES)]
+        w1w_raw = sb("w1w_raw", [P, PASSES * 2 * H], U8)
+        w1s_raw = sb("w1s_raw", [P, PASSES * H], U8)
+        w1w = sb("w1w", [P, PASSES * 2 * H], U8)
+        w1s = sb("w1s", [P, PASSES * H], U8)
+        w2w = sb("w2w", [P, 2 * N], U8)
+        w2s = sb("w2s", [P, N], U8)
+        unit_sb = sb("unit_sb", [P, PACK], F32)
+        xs_both = sb("xs_both", [P, S], U8)
+        xs_second = sb("xs_second", [P, S], U8)
+
+        for plane in (xs_table, w1s_raw, xs_second, w2s):
+            nc.gpsimd.memset(plane[:].bitcast(I32), 0)
+
+        nc.sync.dma_start(offs_sb[:], offs)
+        for q in range(QUADS):
+            nc.scalar.dma_start(
+                xs_table[32 * q : 32 * q + 4 * PASSES, :].bitcast(I32),
+                x_scales[:, 4 * q : 4 * q + 4, :].bitcast(I32),
+            )
+        nc.sync.dma_start(
+            w1w_raw[:].bitcast(I32).rearrange("p (o n) -> p o n", o=PASSES),
+            w1_words.bitcast(I32).rearrange("o p n -> p o n"),
+        )
+        for o in range(PASSES):
+            nc.sync.dma_start(xw_table[o][:], x_words[o].rearrange("p n t -> p (n t)").bitcast(I32))
+        for q in range(QUADS):
+            nc.scalar.dma_start(
+                w1s_raw[32 * q : 32 * q + 4, :].bitcast(I32).rearrange("r (o n) -> r o n", o=PASSES),
+                w1_scales[:, 4 * q : 4 * q + 4, :].bitcast(I32).rearrange("o r n -> r o n"),
+            )
+        nc.sync.dma_start(shf_sb[:], shf)
+        nc.sync.dma_start(lag_sb[:], lag)
+
+        nc.vector.tensor_copy(xs_both[:], xs_table[:].indirect(offs_sb[:]))
+        for q in range(QUADS):
+            nc.sync.dma_start(
+                xs_second[32 * q : 32 * q + 4, :].bitcast(I32),
+                xs_both[32 * q + 4 : 32 * q + 8, :].bitcast(I32),
+            )
+        xs_plane = [xs_both, xs_second]
+
+        nc.sync.dma_start(unit_sb[:], unit.rearrange("(p t) o -> p (t o)", t=PACK))
+        nc.sync.dma_start(w2w[:].bitcast(I32), w2_words[0].bitcast(I32))
+        for q in range(QUADS):
+            nc.sync.dma_start(
+                w2s[32 * q : 32 * q + 4, :].bitcast(I32),
+                w2_scales[0, 4 * q : 4 * q + 4, :].bitcast(I32),
+            )
+
+        nc.vector.tensor_copy(
+            w1w[:].bitcast(U16).rearrange("p (o t m) -> p o t m", o=PASSES, t=PACK),
+            w1w_raw[:].bitcast(U16).rearrange("p (o m t) -> p o t m", o=PASSES, t=PACK),
+        )
+        nc.gpsimd.tensor_copy(
+            w1s[:].rearrange("p (o t m) -> p o t m", o=PASSES, t=PACK),
+            w1s_raw[:].rearrange("p (o m t) -> p o t m", o=PASSES, t=PACK),
+        )
+
+        y_win = [sb(f"y_win{t}", [P, S], F32) for t in range(PACK)]
+        y_own = [sb(f"y_own{t}", [P, S], F32) for t in range(PACK)]
+        halves = [slice(h * HALF, (h + 1) * HALF) for h in range(2)]
+        picked = [[sb(f"picked{o}_{h}", [P, HALF], U32) for h in range(2)] for o in range(PASSES)]
+        banks = [[psum.tile([P, HALF], F32, name=f"bank{t}_{h}") for h in range(2)] for t in range(PACK)]
+
+        def product(o, t, h):
+            col = (o * PACK + t) * P
+            nc.tensor.matmul_mx(
+                out=banks[t][h][:],
+                lhsT=w1w[:, 2 * col : 2 * (col + P)].bitcast(FP4X4),
+                lhsT_scale=w1s[:, col : col + P],
+                rhs=picked[o][h][:].bitcast(FP8X4),
+                rhs_scale=xs_plane[o][:, halves[h]],
+                start=(o == 0),
+                stop=(o == PASSES - 1),
+            )
+
+        for o in range(PASSES):
+            for h in range(2):
+                nc.vector.tensor_copy(
+                    picked[o][h][:], xw_table[o][:].bitcast(U32).indirect(entries(offs_sb, h * HALF, HALF))
+                )
+        for h in range(2):
+            for t in range(PACK):
+                product(0, t, h)
+        for t in range(PACK):
+            for h in range(2):
+                product(1, t, h)
+                nc.scalar.copy(y_win[t][:, halves[h]], banks[t][h][:])
+                if t == 0:
+                    nc.vector.tensor_copy(y_own[t][:, halves[h]], banks[t][h][:])
+                else:
+                    nc.sync.dma_start(y_own[t][:, halves[h]], y_win[t][:, halves[h]])
+
+        lw_sb = keep.tile([P, PACK * U], F32, name="lw_sb", tag="wide0", align_bytes=64)
+        nc.sync.dma_start(lw_sb[:], lw.rearrange("(p t) r -> p (t r)", t=PACK))
+        dif = [sb(f"dif{t}", [P, S], F32) for t in range(PACK)]
+        root = [sb(f"root{t}", [P, S], F32) for t in range(PACK)]
+        q_win = [sb(f"q_win{t}", [P, V + 2 * V], F32) for t in range(PACK)]
+        b_win = [sb(f"b_win{t}", [P, 2 * V], F32) for t in range(PACK)]
+        q_lag = [sb(f"q_lag{t}", [P, U], F32) for t in range(PACK)]
+        poly = sb("poly", [P, PACK * U], F32)
+
+        def differences(t):
+            for h in range(2):
+                cols = slice(h * HALF, (h + 1) * HALF)
+                nc.vector.tensor_tensor(
+                    dif[t][:, cols], y_win[t][:].indirect(entries(shf_sb, h * HALF, HALF)), y_own[t][:, cols], ALU.subtract
+                )
+
+        def roots(t):
+            for h in range(2):
+                cols = slice(h * HALF, (h + 1) * HALF)
+                nc.scalar.activation(y_own[t][:, cols], dif[t][:, cols], ACT.Abs)
+            for h in range(2):
+                cols = slice(h * HALF, (h + 1) * HALF)
+                nc.scalar.activation(root[t][:, cols], y_own[t][:, cols], ACT.Sqrt, bias=0.05 / 16, scale=1.0 / 16)
+
+        def means(t):
+            quads = root[t][:].rearrange("p (v d) -> p v d", d=D)
+            pairs = q_win[t][:, V:].rearrange("p (v e) -> p v e", e=2)
+            nc.vector.tensor_tensor(pairs, quads[:, :, 0:2], quads[:, :, 2:4], ALU.add)
+            nc.vector.tensor_tensor(b_win[t][:, V:], pairs[:, :, 0], pairs[:, :, 1], ALU.add)
+
+        def squares(t):
+            nc.scalar.activation(q_win[t][:, :V], b_win[t][:, V:], ACT.Square)
+            nc.scalar.activation(q_lag[t][:], q_win[t][:].indirect(lag_sb[:]), ACT.Copy)
+
+        def polynomial(t):
+            mine = poly[:, t * U : (t + 1) * U]
+            nc.vector.tensor_tensor(mine, q_lag[t][:], lw_sb[:, t * U : (t + 1) * U], ALU.mult)
+            nc.vector.scalar_tensor_tensor(mine, mine, 0.1, q_lag[t][:], ALU.add, ALU.mult)
+
+        differences(0)
+        roots(0)
+        for t in range(1, PACK):
+            differences(t)
+            roots(t)
+            means(t - 1)
+        means(PACK - 1)
+        for t in range(PACK):
+            squares(t)
+            polynomial(t)
+
+        ln_z = root[PACK - 1]
+        for t in range(PACK):
+            mine = ln_z[:, t * V : (t + 1) * V]
+            nc.scalar.activation(mine, q_win[t][:, :V], ACT.Ln, bias=0.6, scale=0.5)
+            nc.vector.tensor_tensor(b_win[t][:, :V], b_win[t][:, V:], mine, ALU.subtract)
+
+        unit_wide = unit_sb[:].unsqueeze(1).unsqueeze(3).to_broadcast([P, RHALF // 4, PACK, 4])
+        for h in range(2):
+            ln_poly = sb(f"ln_poly{h}", [P, PACK * RHALF], F32)
+            nc.scalar.activation(
+                ln_poly[:].rearrange("p (t r) -> p t r", t=PACK),
+                poly[:].rearrange("p (t r) -> p t r", t=PACK)[:, :, h * RHALF : (h + 1) * RHALF],
+                ACT.Ln,
+                bias=0.12,
+            )
+            total = sb(f"total{h}", [P, PACK * RHALF], F32)
+            for t in range(PACK):
+                cols = slice(t * RHALF, (t + 1) * RHALF)
+                nc.vector.tensor_tensor(
+                    total[:, cols], b_win[t][:].indirect(entries(lag_sb, h * RHALF, RHALF)), ln_poly[:, cols], ALU.add
+                )
+            hid = sb(f"hid{h}", [P, RHALF * PACK], BF16)
+            nc.vector.tensor_tensor(
+                hid[:].rearrange("p (c i t) -> p c t i", i=4, t=PACK),
+                total[:].rearrange("p (t c i) -> p c t i", t=PACK, i=4),
+                unit_wide,
+                ALU.mult,
+            )
+            codes = sb(f"codes{h}", [P, RHALF], U32)
+            scales = sb(f"scales{h}", [P, RHALF], U8)
+            nc.vector.quantize_mx(out=codes[:].bitcast(FP8X4), scales=scales[:], in_=hid[:])
+            fit = psum.tile([P, HALF], F32, name=f"bank0_{h}")
+            nc.tensor.matmul_mx(
+                out=fit[:, :RHALF],
+                lhsT=w2w[:].bitcast(FP4X4),
+                lhsT_scale=w2s[:],
+                rhs=codes[:].bitcast(FP8X4),
+                rhs_scale=scales[:],
+                start=True,
+                stop=True,
+            )
+            result = sb(f"result{h}", [P, RHALF], F32)
+            nc.scalar.copy(result[:], fit[:, :RHALF])
+            nc.sync.dma_start(out[:, h * RHALF : (h + 1) * RHALF], result[:])

@@ -1,6 +1,7 @@
 from contextlib import ExitStack
 
 import concourse.mybir as mybir
+from concourse.masks import make_identity
 
 K, T, S, D, N, H, V, U = 1024, 2048, 1024, 4, 128, 512, 256, 512
 FLOPS = 2 * K * H * S + 2 * H * N * U
@@ -23,6 +24,9 @@ QUADS = 4
 HALF = S // 2
 RHALF = U // 2
 LIST_ROWS = 16
+SPARE = 16
+ABS_ON_VECTOR = ()
+LAG_ON_VECTOR = ((0, 0), (0, 1))
 
 
 def tile_picked_yvario_log_p_kernel(
@@ -42,27 +46,31 @@ def tile_picked_yvario_log_p_kernel(
         offs_sb = sb("offs_sb", [P, S // LIST_ROWS], U16)
         shf_sb = sb("shf_sb", [P, S // LIST_ROWS], U16)
         lag_sb = sb("lag_sb", [P, U // LIST_ROWS], U16)
-        xs_table = sb("xs_table", [P, T], U8)
+        xs_table = keep.tile([P, T], U8, name="xs_table", tag="small_table", align_bytes=64)
         xw_table = [keep.tile([P, T], I32, name=f"xw_table{o}", tag=f"wide{o}", align_bytes=64) for o in range(PASSES)]
-        w1w_raw = sb("w1w_raw", [P, PASSES * 2 * H], U8)
-        w1s_raw = sb("w1s_raw", [P, PASSES * H], U8)
+        w1w_raw = keep.tile([P, PASSES * 2 * H], U8, name="w1w_raw", tag="weight_words", align_bytes=64)
+        w1s_raw = keep.tile([P, PASSES * H], U8, name="w1s_raw", tag="weight_scales", align_bytes=64)
         w1w = sb("w1w", [P, PASSES * 2 * H], U8)
         w1s = sb("w1s", [P, PASSES * H], U8)
-        w2w = sb("w2w", [P, 2 * N], U8)
-        w2s = sb("w2s", [P, N], U8)
-        unit_sb = sb("unit_sb", [P, PACK], F32)
-        xs_both = sb("xs_both", [P, S], U8)
-        xs_second = sb("xs_second", [P, S], U8)
+        xs_picked = sb("xs_picked", [P, S], U8)
+        xs_plane = [sb(f"xs_plane{o}", [P, S], U8) for o in range(PASSES)]
 
-        for plane in (xs_table, w1s_raw, xs_second, w2s):
-            nc.gpsimd.memset(plane[:].bitcast(I32), 0)
+        warm = sb("warm", [P, 2], F32)
+        nc.vector.memset(warm[:, 0:1], 1.0)
+        nc.scalar.activation(warm[:, 1:2], warm[:, 0:1], ACT.Sqrt)
+
+        for first, last in ((32, 64), (64, P)):
+            nc.vector.memset(xs_table[first:last, :].bitcast(I32), 0)
+        for plane in xs_plane:
+            nc.vector.memset(plane[:].bitcast(I32), 0)
+        nc.gpsimd.memset(w1s_raw[:].bitcast(I32), 0)
+        q_win = [sb(f"q_win{t}", [P, V + SPARE], F32) for t in range(PACK)]
+        b_win = [sb(f"b_win{t}", [P, V + SPARE], F32) for t in range(PACK)]
+        for window in q_win + b_win:
+            nc.vector.memset(window[:, V:], 0.0)
 
         nc.sync.dma_start(offs_sb[:], offs)
-        for q in range(QUADS):
-            nc.scalar.dma_start(
-                xs_table[32 * q : 32 * q + 4 * PASSES, :].bitcast(I32),
-                x_scales[:, 4 * q : 4 * q + 4, :].bitcast(I32),
-            )
+        nc.sync.dma_start(xs_table[0:32, :].bitcast(I32), x_scales.bitcast(I32).rearrange("o r n -> (o r) n"))
         nc.sync.dma_start(
             w1w_raw[:].bitcast(I32).rearrange("p (o n) -> p o n", o=PASSES),
             w1_words.bitcast(I32).rearrange("o p n -> p o n"),
@@ -70,34 +78,28 @@ def tile_picked_yvario_log_p_kernel(
         for o in range(PASSES):
             nc.sync.dma_start(xw_table[o][:], x_words[o].rearrange("p n t -> p (n t)").bitcast(I32))
         for q in range(QUADS):
-            nc.scalar.dma_start(
+            nc.gpsimd.dma_start(
                 w1s_raw[32 * q : 32 * q + 4, :].bitcast(I32).rearrange("r (o n) -> r o n", o=PASSES),
                 w1_scales[:, 4 * q : 4 * q + 4, :].bitcast(I32).rearrange("o r n -> r o n"),
             )
         nc.sync.dma_start(shf_sb[:], shf)
         nc.sync.dma_start(lag_sb[:], lag)
 
-        nc.vector.tensor_copy(xs_both[:], xs_table[:].indirect(offs_sb[:]))
-        for q in range(QUADS):
-            nc.sync.dma_start(
-                xs_second[32 * q : 32 * q + 4, :].bitcast(I32),
-                xs_both[32 * q + 4 : 32 * q + 8, :].bitcast(I32),
-            )
-        xs_plane = [xs_both, xs_second]
-
-        nc.sync.dma_start(unit_sb[:], unit.rearrange("(p t) o -> p (t o)", t=PACK))
-        nc.sync.dma_start(w2w[:].bitcast(I32), w2_words[0].bitcast(I32))
-        for q in range(QUADS):
-            nc.sync.dma_start(
-                w2s[32 * q : 32 * q + 4, :].bitcast(I32),
-                w2_scales[0, 4 * q : 4 * q + 4, :].bitcast(I32),
-            )
+        identity = sb("identity", [P, P], F32)
+        make_identity(nc, identity[:])
+        nc.vector.tensor_copy(xs_picked[:], xs_table[:].indirect(offs_sb[:]))
+        for o in range(PASSES):
+            for q in range(QUADS):
+                row = 16 * o + 4 * q
+                nc.sync.dma_start(
+                    xs_plane[o][32 * q : 32 * q + 4, :].bitcast(I32), xs_picked[row : row + 4, :].bitcast(I32)
+                )
 
         nc.vector.tensor_copy(
             w1w[:].bitcast(U16).rearrange("p (o t m) -> p o t m", o=PASSES, t=PACK),
             w1w_raw[:].bitcast(U16).rearrange("p (o m t) -> p o t m", o=PASSES, t=PACK),
         )
-        nc.gpsimd.tensor_copy(
+        nc.vector.tensor_copy(
             w1s[:].rearrange("p (o t m) -> p o t m", o=PASSES, t=PACK),
             w1s_raw[:].rearrange("p (o m t) -> p o t m", o=PASSES, t=PACK),
         )
@@ -125,11 +127,13 @@ def tile_picked_yvario_log_p_kernel(
                 nc.vector.tensor_copy(
                     picked[o][h][:], xw_table[o][:].bitcast(U32).indirect(entries(offs_sb, h * HALF, HALF))
                 )
-        for h in range(2):
-            for t in range(PACK):
+        for t in range(2):
+            for h in range(2):
                 product(0, t, h)
         for t in range(PACK):
             for h in range(2):
+                if t >= 2:
+                    product(0, t, h)
                 product(1, t, h)
                 nc.scalar.copy(y_win[t][:, halves[h]], banks[t][h][:])
                 if t == 0:
@@ -139,12 +143,20 @@ def tile_picked_yvario_log_p_kernel(
 
         lw_sb = keep.tile([P, PACK * U], F32, name="lw_sb", tag="wide0", align_bytes=64)
         nc.sync.dma_start(lw_sb[:], lw.rearrange("(p t) r -> p (t r)", t=PACK))
+        unit_sb = keep.tile([P, PACK], F32, name="unit_sb", tag="small_table", align_bytes=64)
+        nc.sync.dma_start(unit_sb[:], unit.rearrange("(p t) o -> p (t o)", t=PACK))
+        w2w = keep.tile([P, 2 * N], U8, name="w2w", tag="weight_words", align_bytes=64)
+        nc.sync.dma_start(w2w[:].bitcast(I32), w2_words[0].bitcast(I32))
+        w2s = keep.tile([P, N], U8, name="w2s", tag="weight_scales", align_bytes=64)
+        nc.gpsimd.memset(w2s[:].bitcast(I32), 0)
+        for q in range(QUADS):
+            nc.gpsimd.dma_start(
+                w2s[32 * q : 32 * q + 4, :].bitcast(I32),
+                w2_scales[0, 4 * q : 4 * q + 4, :].bitcast(I32),
+            )
         dif = [sb(f"dif{t}", [P, S], F32) for t in range(PACK)]
-        root = [sb(f"root{t}", [P, S], F32) for t in range(PACK)]
-        q_win = [sb(f"q_win{t}", [P, V + 2 * V], F32) for t in range(PACK)]
-        b_win = [sb(f"b_win{t}", [P, 2 * V], F32) for t in range(PACK)]
         q_lag = [sb(f"q_lag{t}", [P, U], F32) for t in range(PACK)]
-        poly = sb("poly", [P, PACK * U], F32)
+        poly = [sb(f"poly{h}", [P, PACK * RHALF], F32) for h in range(2)]
 
         def differences(t):
             for h in range(2):
@@ -153,55 +165,67 @@ def tile_picked_yvario_log_p_kernel(
                     dif[t][:, cols], y_win[t][:].indirect(entries(shf_sb, h * HALF, HALF)), y_own[t][:, cols], ALU.subtract
                 )
 
+        def magnitudes(t, h):
+            by_member = y_own[t][:, halves[h]].rearrange("p (d v) -> p v d", d=D)
+            source = dif[t][:, halves[h]].rearrange("p (v d) -> p v d", d=D)
+            if (t, h) in ABS_ON_VECTOR:
+                nc.vector.scalar_tensor_tensor(by_member, source, -1.0, source, ALU.mult, ALU.max)
+            else:
+                nc.scalar.activation(by_member, source, ACT.Abs)
+            turned = psum.tile([P, HALF], F32, name=f"bank{t}_{h}")
+            for d in range(D):
+                first = h * HALF + d * P
+                nc.tensor.transpose(turned[:, d * P : (d + 1) * P], y_own[t][:, first : first + P], identity[:])
+            return turned
+
         def roots(t):
+            turned = [magnitudes(t, h) for h in range(2)]
+            root = [keep.tile([P, HALF], F32, name=f"root{t}_{h}", tag=f"root{t}_{h}", align_bytes=64) for h in range(2)]
+            nc.scalar.activation(root[0][:], turned[0][:], ACT.Sqrt, bias=0.05 / 16, scale=1.0 / 16)
+            mean = psum.tile([P, HALF], F32, name=f"bank{t}_0")
+            nc.scalar.activation(root[1][:], turned[1][:], ACT.Sqrt, bias=0.05 / 16, scale=1.0 / 16)
             for h in range(2):
-                cols = slice(h * HALF, (h + 1) * HALF)
-                nc.scalar.activation(y_own[t][:, cols], dif[t][:, cols], ACT.Abs)
-            for h in range(2):
-                cols = slice(h * HALF, (h + 1) * HALF)
-                nc.scalar.activation(root[t][:, cols], y_own[t][:, cols], ACT.Sqrt, bias=0.05 / 16, scale=1.0 / 16)
+                for d in range(D):
+                    nc.tensor.matmul(
+                        mean[:, h * P : (h + 1) * P],
+                        root[h][:, d * P : (d + 1) * P],
+                        identity[:],
+                        start=(d == 0),
+                        stop=(d == D - 1),
+                        is_transpose=True,
+                    )
+            return mean
 
-        def means(t):
-            quads = root[t][:].rearrange("p (v d) -> p v d", d=D)
-            pairs = q_win[t][:, V:].rearrange("p (v e) -> p v e", e=2)
-            nc.vector.tensor_tensor(pairs, quads[:, :, 0:2], quads[:, :, 2:4], ALU.add)
-            nc.vector.tensor_tensor(b_win[t][:, V:], pairs[:, :, 0], pairs[:, :, 1], ALU.add)
+        def polynomial(t, h):
+            cols = slice(h * RHALF, (h + 1) * RHALF)
+            mine = poly[h][:, t * RHALF : (t + 1) * RHALF]
+            looked_up = q_win[t][:].indirect(entries(lag_sb, h * RHALF, RHALF))
+            if (t, h) in LAG_ON_VECTOR:
+                nc.vector.tensor_copy(q_lag[t][:, cols], looked_up)
+            else:
+                nc.scalar.activation(q_lag[t][:, cols], looked_up, ACT.Copy)
+            nc.vector.tensor_tensor(mine, q_lag[t][:, cols], lw_sb[:, t * U + h * RHALF : t * U + (h + 1) * RHALF], ALU.mult)
+            nc.vector.scalar_tensor_tensor(mine, mine, 0.1, q_lag[t][:, cols], ALU.add, ALU.mult)
 
-        def squares(t):
-            nc.scalar.activation(q_win[t][:, :V], b_win[t][:, V:], ACT.Square)
-            nc.scalar.activation(q_lag[t][:], q_win[t][:].indirect(lag_sb[:]), ACT.Copy)
-
-        def polynomial(t):
-            mine = poly[:, t * U : (t + 1) * U]
-            nc.vector.tensor_tensor(mine, q_lag[t][:], lw_sb[:, t * U : (t + 1) * U], ALU.mult)
-            nc.vector.scalar_tensor_tensor(mine, mine, 0.1, q_lag[t][:], ALU.add, ALU.mult)
-
-        differences(0)
-        roots(0)
-        for t in range(1, PACK):
-            differences(t)
-            roots(t)
-            means(t - 1)
-        means(PACK - 1)
+        rmean = []
         for t in range(PACK):
-            squares(t)
-            polynomial(t)
+            differences(t)
+            rmean.append(roots(t))
+            nc.scalar.activation(q_win[t][:, :V], rmean[t][:, :V], ACT.Square)
+        for t in range(PACK):
+            for h in range(2):
+                polynomial(t, h)
 
-        ln_z = root[PACK - 1]
+        ln_z = keep.tile([P, PACK * V], F32, name="ln_z", tag=f"root{PACK - 1}_1", align_bytes=64)
         for t in range(PACK):
             mine = ln_z[:, t * V : (t + 1) * V]
             nc.scalar.activation(mine, q_win[t][:, :V], ACT.Ln, bias=0.6, scale=0.5)
-            nc.vector.tensor_tensor(b_win[t][:, :V], b_win[t][:, V:], mine, ALU.subtract)
+            nc.vector.tensor_tensor(b_win[t][:, :V], rmean[t][:, :V], mine, ALU.subtract)
 
         unit_wide = unit_sb[:].unsqueeze(1).unsqueeze(3).to_broadcast([P, RHALF // 4, PACK, 4])
         for h in range(2):
             ln_poly = sb(f"ln_poly{h}", [P, PACK * RHALF], F32)
-            nc.scalar.activation(
-                ln_poly[:].rearrange("p (t r) -> p t r", t=PACK),
-                poly[:].rearrange("p (t r) -> p t r", t=PACK)[:, :, h * RHALF : (h + 1) * RHALF],
-                ACT.Ln,
-                bias=0.12,
-            )
+            nc.scalar.activation(ln_poly[:], poly[h][:], ACT.Ln, bias=0.12)
             total = sb(f"total{h}", [P, PACK * RHALF], F32)
             for t in range(PACK):
                 cols = slice(t * RHALF, (t + 1) * RHALF)
@@ -218,7 +242,7 @@ def tile_picked_yvario_log_p_kernel(
             codes = sb(f"codes{h}", [P, RHALF], U32)
             scales = sb(f"scales{h}", [P, RHALF], U8)
             nc.vector.quantize_mx(out=codes[:].bitcast(FP8X4), scales=scales[:], in_=hid[:])
-            fit = psum.tile([P, HALF], F32, name=f"bank0_{h}")
+            fit = psum.tile([P, HALF], F32, name=f"bank{h}_1")
             nc.tensor.matmul_mx(
                 out=fit[:, :RHALF],
                 lhsT=w2w[:].bitcast(FP4X4),

@@ -25,8 +25,9 @@ HALF = S // 2
 RHALF = U // 2
 LIST_ROWS = 16
 SPARE = 16
+B_ON_SCALAR = 4
 ABS_ON_VECTOR = ()
-LAG_ON_VECTOR = ((0, 0), (0, 1))
+LAG_ON_VECTOR = ((0, 0), (1, 0), (2, 0), (0, 1), (1, 1), (2, 1))
 
 
 def tile_picked_yvario_log_p_kernel(
@@ -75,15 +76,16 @@ def tile_picked_yvario_log_p_kernel(
             w1w_raw[:].bitcast(I32).rearrange("p (o n) -> p o n", o=PASSES),
             w1_words.bitcast(I32).rearrange("o p n -> p o n"),
         )
-        for o in range(PASSES):
-            nc.sync.dma_start(xw_table[o][:], x_words[o].rearrange("p n t -> p (n t)").bitcast(I32))
+        nc.sync.dma_start(xw_table[0][:], x_words[0].rearrange("p n t -> p (n t)").bitcast(I32))
+        nc.sync.dma_start(shf_sb[:], shf)
+        nc.sync.dma_start(lag_sb[:], lag)
+        nc.sync.dma_start(xw_table[1][:], x_words[1].rearrange("p n t -> p (n t)").bitcast(I32))
         for q in range(QUADS):
-            nc.gpsimd.dma_start(
+            queue = nc.gpsimd if q < QUADS // 2 else nc.scalar
+            queue.dma_start(
                 w1s_raw[32 * q : 32 * q + 4, :].bitcast(I32).rearrange("r (o n) -> r o n", o=PASSES),
                 w1_scales[:, 4 * q : 4 * q + 4, :].bitcast(I32).rearrange("o r n -> r o n"),
             )
-        nc.sync.dma_start(shf_sb[:], shf)
-        nc.sync.dma_start(lag_sb[:], lag)
 
         identity = sb("identity", [P, P], F32)
         make_identity(nc, identity[:])
@@ -150,7 +152,7 @@ def tile_picked_yvario_log_p_kernel(
         w2s = keep.tile([P, N], U8, name="w2s", tag="weight_scales", align_bytes=64)
         nc.gpsimd.memset(w2s[:].bitcast(I32), 0)
         for q in range(QUADS):
-            nc.gpsimd.dma_start(
+            nc.sync.dma_start(
                 w2s[32 * q : 32 * q + 4, :].bitcast(I32),
                 w2_scales[0, 4 * q : 4 * q + 4, :].bitcast(I32),
             )
@@ -196,16 +198,20 @@ def tile_picked_yvario_log_p_kernel(
                     )
             return mean
 
-        def polynomial(t, h):
-            cols = slice(h * RHALF, (h + 1) * RHALF)
-            mine = poly[h][:, t * RHALF : (t + 1) * RHALF]
-            looked_up = q_win[t][:].indirect(entries(lag_sb, h * RHALF, RHALF))
-            if (t, h) in LAG_ON_VECTOR:
-                nc.vector.tensor_copy(q_lag[t][:, cols], looked_up)
-            else:
-                nc.scalar.activation(q_lag[t][:, cols], looked_up, ACT.Copy)
-            nc.vector.tensor_tensor(mine, q_lag[t][:, cols], lw_sb[:, t * U + h * RHALF : t * U + (h + 1) * RHALF], ALU.mult)
-            nc.vector.scalar_tensor_tensor(mine, mine, 0.1, q_lag[t][:, cols], ALU.add, ALU.mult)
+        def polynomial(t):
+            looked = [q_lag[t][:, h * RHALF : (h + 1) * RHALF] for h in range(2)]
+            mine = [poly[h][:, t * RHALF : (t + 1) * RHALF] for h in range(2)]
+            for h in range(2):
+                window = q_win[t][:].indirect(entries(lag_sb, h * RHALF, RHALF))
+                if (t, h) in LAG_ON_VECTOR:
+                    nc.vector.tensor_copy(looked[h], window)
+                else:
+                    nc.scalar.activation(looked[h], window, ACT.Copy)
+            for h in range(2):
+                first = t * U + h * RHALF
+                nc.vector.tensor_tensor(mine[h], looked[h], lw_sb[:, first : first + RHALF], ALU.mult)
+            for h in range(2):
+                nc.vector.scalar_tensor_tensor(mine[h], mine[h], 0.1, looked[h], ALU.add, ALU.mult)
 
         rmean = []
         for t in range(PACK):
@@ -213,8 +219,7 @@ def tile_picked_yvario_log_p_kernel(
             rmean.append(roots(t))
             nc.scalar.activation(q_win[t][:, :V], rmean[t][:, :V], ACT.Square)
         for t in range(PACK):
-            for h in range(2):
-                polynomial(t, h)
+            polynomial(t)
 
         ln_z = keep.tile([P, PACK * V], F32, name="ln_z", tag=f"root{PACK - 1}_1", align_bytes=64)
         for t in range(PACK):
@@ -222,26 +227,26 @@ def tile_picked_yvario_log_p_kernel(
             nc.scalar.activation(mine, q_win[t][:, :V], ACT.Ln, bias=0.6, scale=0.5)
             nc.vector.tensor_tensor(b_win[t][:, :V], rmean[t][:, :V], mine, ALU.subtract)
 
+        ln_poly = [sb(f"ln_poly{h}", [P, PACK * RHALF], F32) for h in range(2)]
+        total = [sb(f"total{h}", [P, PACK * RHALF], F32) for h in range(2)]
+        hid = [sb(f"hid{h}", [P, RHALF * PACK], BF16) for h in range(2)]
         unit_wide = unit_sb[:].unsqueeze(1).unsqueeze(3).to_broadcast([P, RHALF // 4, PACK, 4])
-        for h in range(2):
-            ln_poly = sb(f"ln_poly{h}", [P, PACK * RHALF], F32)
-            nc.scalar.activation(ln_poly[:], poly[h][:], ACT.Ln, bias=0.12)
-            total = sb(f"total{h}", [P, PACK * RHALF], F32)
-            for t in range(PACK):
-                cols = slice(t * RHALF, (t + 1) * RHALF)
-                nc.vector.tensor_tensor(
-                    total[:, cols], b_win[t][:].indirect(entries(lag_sb, h * RHALF, RHALF)), ln_poly[:, cols], ALU.add
-                )
-            hid = sb(f"hid{h}", [P, RHALF * PACK], BF16)
+
+        def b_window(t, h):
+            return b_win[t][:].indirect(entries(lag_sb, h * RHALF, RHALF))
+
+        def scaled(h):
             nc.vector.tensor_tensor(
-                hid[:].rearrange("p (c i t) -> p c t i", i=4, t=PACK),
-                total[:].rearrange("p (t c i) -> p c t i", t=PACK, i=4),
+                hid[h][:].rearrange("p (c i t) -> p c t i", i=4, t=PACK),
+                total[h][:].rearrange("p (t c i) -> p c t i", t=PACK, i=4),
                 unit_wide,
                 ALU.mult,
             )
+
+        def fitted(h):
             codes = sb(f"codes{h}", [P, RHALF], U32)
             scales = sb(f"scales{h}", [P, RHALF], U8)
-            nc.vector.quantize_mx(out=codes[:].bitcast(FP8X4), scales=scales[:], in_=hid[:])
+            nc.vector.quantize_mx(out=codes[:].bitcast(FP8X4), scales=scales[:], in_=hid[h][:])
             fit = psum.tile([P, HALF], F32, name=f"bank{h}_1")
             nc.tensor.matmul_mx(
                 out=fit[:, :RHALF],
@@ -255,3 +260,20 @@ def tile_picked_yvario_log_p_kernel(
             result = sb(f"result{h}", [P, RHALF], F32)
             nc.scalar.copy(result[:], fit[:, :RHALF])
             nc.sync.dma_start(out[:, h * RHALF : (h + 1) * RHALF], result[:])
+
+        tiles = [slice(t * RHALF, (t + 1) * RHALF) for t in range(PACK)]
+        b_lag = sb("b_lag", [P, PACK * RHALF], F32)
+        nc.scalar.activation(ln_poly[0][:], poly[0][:], ACT.Ln, bias=0.12)
+        for t in range(PACK):
+            nc.vector.tensor_tensor(total[0][:, tiles[t]], b_window(t, 0), ln_poly[0][:, tiles[t]], ALU.add)
+        nc.scalar.activation(ln_poly[1][:], poly[1][:], ACT.Ln, bias=0.12)
+        for t in range(B_ON_SCALAR):
+            nc.scalar.activation(b_lag[:, tiles[t]], b_window(t, 1), ACT.Copy)
+        for t in range(B_ON_SCALAR, PACK):
+            nc.vector.tensor_tensor(total[1][:, tiles[t]], b_window(t, 1), ln_poly[1][:, tiles[t]], ALU.add)
+        scaled(0)
+        fetched = slice(0, B_ON_SCALAR * RHALF)
+        nc.vector.tensor_tensor(total[1][:, fetched], b_lag[:, fetched], ln_poly[1][:, fetched], ALU.add)
+        fitted(0)
+        scaled(1)
+        fitted(1)

@@ -25,6 +25,7 @@ HALF = S // 2
 RHALF = U // 2
 LIST_ROWS = 16
 SPARE = 16
+SCALE_ON_SCALAR = (0,)
 B_ON_SCALAR = 4
 ABS_ON_VECTOR = ()
 LAG_ON_VECTOR = ((0, 0), (1, 0), (2, 0), (0, 1), (1, 1), (2, 1))
@@ -48,11 +49,11 @@ def tile_picked_yvario_log_p_kernel(
         shf_sb = sb("shf_sb", [P, S // LIST_ROWS], U16)
         lag_sb = sb("lag_sb", [P, U // LIST_ROWS], U16)
         xs_table = keep.tile([P, T], U8, name="xs_table", tag="small_table", align_bytes=64)
-        xw_table = [keep.tile([P, T], I32, name=f"xw_table{o}", tag=f"wide{o}", align_bytes=64) for o in range(PASSES)]
+        xw_table = [sb(f"xw_table{o}", [P, T], I32) for o in range(PASSES)]
         w1w_raw = keep.tile([P, PASSES * 2 * H], U8, name="w1w_raw", tag="weight_words", align_bytes=64)
-        w1s_raw = keep.tile([P, PASSES * H], U8, name="w1s_raw", tag="weight_scales", align_bytes=64)
+        w1s_raw = keep.tile([P, H], U8, name="w1s_raw", tag="weight_scales", align_bytes=64)
         w1w = sb("w1w", [P, PASSES * 2 * H], U8)
-        w1s = sb("w1s", [P, PASSES * H], U8)
+        w1s_dealt = sb("w1s_dealt", [P, H], U8)
         xs_picked = sb("xs_picked", [P, S], U8)
         xs_plane = [sb(f"xs_plane{o}", [P, S], U8) for o in range(PASSES)]
 
@@ -61,10 +62,10 @@ def tile_picked_yvario_log_p_kernel(
         nc.scalar.activation(warm[:, 1:2], warm[:, 0:1], ACT.Sqrt)
 
         for first, last in ((32, 64), (64, P)):
+            nc.vector.memset(w1s_raw[first:last, :].bitcast(I32), 0)
             nc.vector.memset(xs_table[first:last, :].bitcast(I32), 0)
         for plane in xs_plane:
             nc.vector.memset(plane[:].bitcast(I32), 0)
-        nc.gpsimd.memset(w1s_raw[:].bitcast(I32), 0)
         q_win = [sb(f"q_win{t}", [P, V + SPARE], F32) for t in range(PACK)]
         b_win = [sb(f"b_win{t}", [P, V + SPARE], F32) for t in range(PACK)]
         for window in q_win + b_win:
@@ -72,6 +73,7 @@ def tile_picked_yvario_log_p_kernel(
 
         nc.sync.dma_start(offs_sb[:], offs)
         nc.sync.dma_start(xs_table[0:32, :].bitcast(I32), x_scales.bitcast(I32).rearrange("o r n -> (o r) n"))
+        nc.sync.dma_start(w1s_raw[0:32, :].bitcast(I32), w1_scales.bitcast(I32).rearrange("o r n -> (o r) n"))
         nc.sync.dma_start(
             w1w_raw[:].bitcast(I32).rearrange("p (o n) -> p o n", o=PASSES),
             w1_words.bitcast(I32).rearrange("o p n -> p o n"),
@@ -80,12 +82,13 @@ def tile_picked_yvario_log_p_kernel(
         nc.sync.dma_start(shf_sb[:], shf)
         nc.sync.dma_start(lag_sb[:], lag)
         nc.sync.dma_start(xw_table[1][:], x_words[1].rearrange("p n t -> p (n t)").bitcast(I32))
-        for q in range(QUADS):
-            queue = nc.gpsimd if q < QUADS // 2 else nc.scalar
-            queue.dma_start(
-                w1s_raw[32 * q : 32 * q + 4, :].bitcast(I32).rearrange("r (o n) -> r o n", o=PASSES),
-                w1_scales[:, 4 * q : 4 * q + 4, :].bitcast(I32).rearrange("o r n -> r o n"),
-            )
+
+        nc.vector.tensor_copy(
+            w1s_dealt[:].rearrange("p (t m) -> p t m", t=PACK),
+            w1s_raw[:].rearrange("p (m t) -> p t m", t=PACK),
+        )
+        for q in range(1, QUADS):
+            nc.sync.dma_start(w1s_dealt[32 * q : 32 * q + 4, :].bitcast(I32), w1s_dealt[4 * q : 4 * q + 4, :].bitcast(I32))
 
         identity = sb("identity", [P, P], F32)
         make_identity(nc, identity[:])
@@ -97,19 +100,27 @@ def tile_picked_yvario_log_p_kernel(
                     xs_plane[o][32 * q : 32 * q + 4, :].bitcast(I32), xs_picked[row : row + 4, :].bitcast(I32)
                 )
 
+        w1s_second = keep.tile([P, H], U8, name="w1s_second", tag="small_table", align_bytes=64)
+        nc.gpsimd.memset(w1s_second[:].bitcast(I32), 0)
+        for q in range(QUADS):
+            row = 16 + 4 * q
+            nc.sync.dma_start(
+                w1s_second[32 * q : 32 * q + 4, :].bitcast(I32), w1s_dealt[row : row + 4, :].bitcast(I32)
+            )
+        w1s = [w1s_dealt, w1s_second]
+
         nc.vector.tensor_copy(
             w1w[:].bitcast(U16).rearrange("p (o t m) -> p o t m", o=PASSES, t=PACK),
             w1w_raw[:].bitcast(U16).rearrange("p (o m t) -> p o t m", o=PASSES, t=PACK),
-        )
-        nc.vector.tensor_copy(
-            w1s[:].rearrange("p (o t m) -> p o t m", o=PASSES, t=PACK),
-            w1s_raw[:].rearrange("p (o m t) -> p o t m", o=PASSES, t=PACK),
         )
 
         y_win = [sb(f"y_win{t}", [P, S], F32) for t in range(PACK)]
         y_own = [sb(f"y_own{t}", [P, S], F32) for t in range(PACK)]
         halves = [slice(h * HALF, (h + 1) * HALF) for h in range(2)]
-        picked = [[sb(f"picked{o}_{h}", [P, HALF], U32) for h in range(2)] for o in range(PASSES)]
+        picked = [
+            [keep.tile([P, HALF], U32, name=f"picked{o}_{h}", tag=f"picked{o}_{h}", align_bytes=64) for h in range(2)]
+            for o in range(PASSES)
+        ]
         banks = [[psum.tile([P, HALF], F32, name=f"bank{t}_{h}") for h in range(2)] for t in range(PACK)]
 
         def product(o, t, h):
@@ -117,7 +128,7 @@ def tile_picked_yvario_log_p_kernel(
             nc.tensor.matmul_mx(
                 out=banks[t][h][:],
                 lhsT=w1w[:, 2 * col : 2 * (col + P)].bitcast(FP4X4),
-                lhsT_scale=w1s[:, col : col + P],
+                lhsT_scale=w1s[o][:, t * P : (t + 1) * P],
                 rhs=picked[o][h][:].bitcast(FP8X4),
                 rhs_scale=xs_plane[o][:, halves[h]],
                 start=(o == 0),
@@ -143,7 +154,7 @@ def tile_picked_yvario_log_p_kernel(
                 else:
                     nc.sync.dma_start(y_own[t][:, halves[h]], y_win[t][:, halves[h]])
 
-        lw_sb = keep.tile([P, PACK * U], F32, name="lw_sb", tag="wide0", align_bytes=64)
+        lw_sb = keep.tile([P, PACK * U], F32, name="lw_sb", tag="picked1_1", align_bytes=64)
         nc.sync.dma_start(lw_sb[:], lw.rearrange("(p t) r -> p (t r)", t=PACK))
         unit_sb = keep.tile([P, PACK], F32, name="unit_sb", tag="small_table", align_bytes=64)
         nc.sync.dma_start(unit_sb[:], unit.rearrange("(p t) o -> p (t o)", t=PACK))
@@ -230,17 +241,23 @@ def tile_picked_yvario_log_p_kernel(
         ln_poly = [sb(f"ln_poly{h}", [P, PACK * RHALF], F32) for h in range(2)]
         total = [sb(f"total{h}", [P, PACK * RHALF], F32) for h in range(2)]
         hid = [sb(f"hid{h}", [P, RHALF * PACK], BF16) for h in range(2)]
-        unit_wide = unit_sb[:].unsqueeze(1).unsqueeze(3).to_broadcast([P, RHALF // 4, PACK, 4])
+        rounded = [sb(f"rounded{h}", [P, PACK * RHALF], BF16) for h in range(2)]
 
         def b_window(t, h):
             return b_win[t][:].indirect(entries(lag_sb, h * RHALF, RHALF))
 
         def scaled(h):
-            nc.vector.tensor_tensor(
+            for t in range(PACK):
+                cols = slice(t * RHALF, (t + 1) * RHALF)
+                if h in SCALE_ON_SCALAR:
+                    nc.scalar.activation(rounded[h][:, cols], total[h][:, cols], ACT.Copy, scale=unit_sb[:, t : t + 1])
+                else:
+                    nc.vector.tensor_scalar(rounded[h][:, cols], total[h][:, cols], unit_sb[:, t : t + 1], None, ALU.mult)
+
+        def woven(h):
+            nc.vector.tensor_copy(
                 hid[h][:].rearrange("p (c i t) -> p c t i", i=4, t=PACK),
-                total[h][:].rearrange("p (t c i) -> p c t i", t=PACK, i=4),
-                unit_wide,
-                ALU.mult,
+                rounded[h][:].rearrange("p (t c i) -> p c t i", t=PACK, i=4),
             )
 
         def fitted(h):
@@ -274,6 +291,8 @@ def tile_picked_yvario_log_p_kernel(
         scaled(0)
         fetched = slice(0, B_ON_SCALAR * RHALF)
         nc.vector.tensor_tensor(total[1][:, fetched], b_lag[:, fetched], ln_poly[1][:, fetched], ALU.add)
-        fitted(0)
+        woven(0)
         scaled(1)
+        fitted(0)
+        woven(1)
         fitted(1)

@@ -28,7 +28,7 @@ SPARE = 16
 SCALE_ON_SCALAR = (0,)
 B_ON_SCALAR = 4
 ABS_ON_VECTOR = ()
-LAG_ON_VECTOR = ((0, 0), (1, 0), (2, 0), (0, 1), (1, 1), (2, 1))
+LAG_ON_VECTOR = ((0, 0), (1, 0), (0, 1), (1, 1))
 
 
 def tile_picked_yvario_log_p_kernel(
@@ -254,19 +254,23 @@ def tile_picked_yvario_log_p_kernel(
                 else:
                     nc.vector.tensor_scalar(rounded[h][:, cols], total[h][:, cols], unit_sb[:, t : t + 1], None, ALU.mult)
 
-        def woven(h):
+        def woven(h, first, count):
             nc.vector.tensor_copy(
-                hid[h][:].rearrange("p (c i t) -> p c t i", i=4, t=PACK),
-                rounded[h][:].rearrange("p (t c i) -> p c t i", t=PACK, i=4),
+                hid[h][:, first * PACK : (first + count) * PACK].rearrange("p (c i t) -> p c t i", i=4, t=PACK),
+                rounded[h][:].rearrange("p (t r) -> p t r", t=PACK)[:, :, first : first + count].rearrange(
+                    "p t (c i) -> p c t i", i=4
+                ),
             )
 
-        def fitted(h):
-            codes = sb(f"codes{h}", [P, RHALF], U32)
-            scales = sb(f"scales{h}", [P, RHALF], U8)
-            nc.vector.quantize_mx(out=codes[:].bitcast(FP8X4), scales=scales[:], in_=hid[h][:])
-            fit = psum.tile([P, HALF], F32, name=f"bank{h}_1")
+        def fitted(h, first, count, bank):
+            codes = sb(f"codes{bank}", [P, count], U32)
+            scales = sb(f"scales{bank}", [P, count], U8)
+            nc.vector.quantize_mx(
+                out=codes[:].bitcast(FP8X4), scales=scales[:], in_=hid[h][:, first * PACK : (first + count) * PACK]
+            )
+            fit = psum.tile([P, HALF], F32, name=f"bank{bank}_1")
             nc.tensor.matmul_mx(
-                out=fit[:, :RHALF],
+                out=fit[:, :count],
                 lhsT=w2w[:].bitcast(FP4X4),
                 lhsT_scale=w2s[:],
                 rhs=codes[:].bitcast(FP8X4),
@@ -274,9 +278,10 @@ def tile_picked_yvario_log_p_kernel(
                 start=True,
                 stop=True,
             )
-            result = sb(f"result{h}", [P, RHALF], F32)
-            nc.scalar.copy(result[:], fit[:, :RHALF])
-            nc.sync.dma_start(out[:, h * RHALF : (h + 1) * RHALF], result[:])
+            result = sb(f"result{bank}", [P, count], F32)
+            nc.scalar.copy(result[:], fit[:, :count])
+            column = h * RHALF + first
+            nc.sync.dma_start(out[:, column : column + count], result[:])
 
         tiles = [slice(t * RHALF, (t + 1) * RHALF) for t in range(PACK)]
         b_lag = sb("b_lag", [P, PACK * RHALF], F32)
@@ -291,8 +296,11 @@ def tile_picked_yvario_log_p_kernel(
         scaled(0)
         fetched = slice(0, B_ON_SCALAR * RHALF)
         nc.vector.tensor_tensor(total[1][:, fetched], b_lag[:, fetched], ln_poly[1][:, fetched], ALU.add)
-        woven(0)
+        woven(0, 0, RHALF)
         scaled(1)
-        fitted(0)
-        woven(1)
-        fitted(1)
+        fitted(0, 0, RHALF, 0)
+        quarter = RHALF // 2
+        woven(1, 0, quarter)
+        woven(1, quarter, quarter)
+        fitted(1, 0, quarter, 1)
+        fitted(1, quarter, quarter, 2)

from contextlib import ExitStack

import concourse.mybir as mybir
from concourse.masks import make_identity

K, T, S, D, N, H, V, U = 1024, 2048, 1024, 4, 128, 512, 256, 512
FLOPS = 2 * K * H * S + 2 * H * N * U

F32 = mybir.dt.float32
BF16 = mybir.dt.bfloat16
I32 = mybir.dt.int32
U32 = mybir.dt.uint32
U16 = mybir.dt.uint16
U8 = mybir.dt.uint8
FP8X4 = mybir.dt.float8_e4m3fn_x4
FP4X4 = mybir.dt.float4_e2m1fn_x4
ALU = mybir.AluOpType
ACT = mybir.ActivationFunctionType

P = 128
PACK = 4
PASSES = K // (P * PACK)
QUADS = 4
HALF = S // 2
RHALF = U // 2
LIST_ROWS = 16
SPARE = 16
SCALE_ON_SCALAR = (0,)
B_ON_SCALAR = 4
ABS_ON_VECTOR = ()
LAG_ON_VECTOR = ((0, 0), (1, 0), (0, 1), (1, 1))


def tile_picked_yvario_log_p_kernel(
    tc, x_words, x_scales, w1_words, w1_scales, lw, unit, w2_words, w2_scales, offs, shf, lag, out
):
    nc = tc.nc
    with ExitStack() as ctx:
        keep = ctx.enter_context(tc.tile_pool(name="keep", bufs=1))
        psum = ctx.enter_context(tc.psum_pool(name="psum", bufs=1))

        def sb(name, shape, dtype):
            return keep.tile(shape, dtype, name=name, align_bytes=64)

        def entries(list_tile, first, count):
            return list_tile[:, first // LIST_ROWS : (first + count) // LIST_ROWS]

        offs_sb = sb("offs_sb", [P, S // LIST_ROWS], U16)
        shf_sb = sb("shf_sb", [P, S // LIST_ROWS], U16)
        lag_sb = sb("lag_sb", [P, U // LIST_ROWS], U16)
        xs_table = keep.tile([P, T], U8, name="xs_table", tag="small_table", align_bytes=64)
        xw_table = [sb(f"xw_table{o}", [P, T], I32) for o in range(PASSES)]
        w1w_raw = keep.tile([P, PASSES * 2 * H], U8, name="w1w_raw", tag="weight_words", align_bytes=64)
        w1s_raw = keep.tile([P, H], U8, name="w1s_raw", tag="weight_scales", align_bytes=64)
        w1w = sb("w1w", [P, PASSES * 2 * H], U8)
        w1s_dealt = sb("w1s_dealt", [P, H], U8)
        xs_picked = sb("xs_picked", [P, S], U8)
        xs_plane = [sb(f"xs_plane{o}", [P, S], U8) for o in range(PASSES)]

        warm = sb("warm", [P, 2], F32)
        nc.vector.memset(warm[:, 0:1], 1.0)
        nc.scalar.activation(warm[:, 1:2], warm[:, 0:1], ACT.Sqrt)

        for first, last in ((32, 64), (64, P)):
            nc.vector.memset(w1s_raw[first:last, :].bitcast(I32), 0)
            nc.vector.memset(xs_table[first:last, :].bitcast(I32), 0)
        for plane in xs_plane:
            nc.vector.memset(plane[:].bitcast(I32), 0)
        q_win = [sb(f"q_win{t}", [P, V + SPARE], F32) for t in range(PACK)]
        b_win = [sb(f"b_win{t}", [P, V + SPARE], F32) for t in range(PACK)]
        for window in q_win + b_win:
            nc.vector.memset(window[:, V:], 0.0)

        nc.sync.dma_start(offs_sb[:], offs)
        nc.sync.dma_start(xs_table[0:32, :].bitcast(I32), x_scales.bitcast(I32).rearrange("o r n -> (o r) n"))
        nc.sync.dma_start(w1s_raw[0:32, :].bitcast(I32), w1_scales.bitcast(I32).rearrange("o r n -> (o r) n"))
        nc.sync.dma_start(
            w1w_raw[:].bitcast(I32).rearrange("p (o n) -> p o n", o=PASSES),
            w1_words.bitcast(I32).rearrange("o p n -> p o n"),
        )
        nc.sync.dma_start(xw_table[0][:], x_words[0].rearrange("p n t -> p (n t)").bitcast(I32))
        nc.sync.dma_start(shf_sb[:], shf)
        nc.sync.dma_start(lag_sb[:], lag)
        nc.sync.dma_start(xw_table[1][:], x_words[1].rearrange("p n t -> p (n t)").bitcast(I32))

        nc.vector.tensor_copy(
            w1s_dealt[:].rearrange("p (t m) -> p t m", t=PACK),
            w1s_raw[:].rearrange("p (m t) -> p t m", t=PACK),
        )
        for q in range(1, QUADS):
            nc.sync.dma_start(w1s_dealt[32 * q : 32 * q + 4, :].bitcast(I32), w1s_dealt[4 * q : 4 * q + 4, :].bitcast(I32))

        identity = sb("identity", [P, P], F32)
        make_identity(nc, identity[:])
        nc.vector.tensor_copy(xs_picked[:], xs_table[:].indirect(offs_sb[:]))
        for o in range(PASSES):
            for q in range(QUADS):
                row = 16 * o + 4 * q
                nc.sync.dma_start(
                    xs_plane[o][32 * q : 32 * q + 4, :].bitcast(I32), xs_picked[row : row + 4, :].bitcast(I32)
                )

        w1s_second = keep.tile([P, H], U8, name="w1s_second", tag="small_table", align_bytes=64)
        nc.gpsimd.memset(w1s_second[:].bitcast(I32), 0)
        for q in range(QUADS):
            row = 16 + 4 * q
            nc.sync.dma_start(
                w1s_second[32 * q : 32 * q + 4, :].bitcast(I32), w1s_dealt[row : row + 4, :].bitcast(I32)
            )
        w1s = [w1s_dealt, w1s_second]

        nc.vector.tensor_copy(
            w1w[:].bitcast(U16).rearrange("p (o t m) -> p o t m", o=PASSES, t=PACK),
            w1w_raw[:].bitcast(U16).rearrange("p (o m t) -> p o t m", o=PASSES, t=PACK),
        )

        y_win = [sb(f"y_win{t}", [P, S], F32) for t in range(PACK)]
        y_own = [sb(f"y_own{t}", [P, S], F32) for t in range(PACK)]
        halves = [slice(h * HALF, (h + 1) * HALF) for h in range(2)]
        picked = [
            [keep.tile([P, HALF], U32, name=f"picked{o}_{h}", tag=f"picked{o}_{h}", align_bytes=64) for h in range(2)]
            for o in range(PASSES)
        ]
        banks = [[psum.tile([P, HALF], F32, name=f"bank{t}_{h}") for h in range(2)] for t in range(PACK)]

        def product(o, t, h):
            col = (o * PACK + t) * P
            nc.tensor.matmul_mx(
                out=banks[t][h][:],
                lhsT=w1w[:, 2 * col : 2 * (col + P)].bitcast(FP4X4),
                lhsT_scale=w1s[o][:, t * P : (t + 1) * P],
                rhs=picked[o][h][:].bitcast(FP8X4),
                rhs_scale=xs_plane[o][:, halves[h]],
                start=(o == 0),
                stop=(o == PASSES - 1),
            )

        for o in range(PASSES):
            for h in range(2):
                nc.vector.tensor_copy(
                    picked[o][h][:], xw_table[o][:].bitcast(U32).indirect(entries(offs_sb, h * HALF, HALF))
                )
        for t in range(2):
            for h in range(2):
                product(0, t, h)
        for t in range(PACK):
            for h in range(2):
                if t >= 2:
                    product(0, t, h)
                product(1, t, h)
                nc.scalar.copy(y_win[t][:, halves[h]], banks[t][h][:])
                if t == 0:
                    nc.vector.tensor_copy(y_own[t][:, halves[h]], banks[t][h][:])
                else:
                    nc.sync.dma_start(y_own[t][:, halves[h]], y_win[t][:, halves[h]])

        lw_sb = keep.tile([P, PACK * U], F32, name="lw_sb", tag="picked1_1", align_bytes=64)
        nc.sync.dma_start(lw_sb[:], lw.rearrange("(p t) r -> p (t r)", t=PACK))
        unit_sb = keep.tile([P, PACK], F32, name="unit_sb", tag="small_table", align_bytes=64)
        nc.sync.dma_start(unit_sb[:], unit.rearrange("(p t) o -> p (t o)", t=PACK))
        w2w = keep.tile([P, 2 * N], U8, name="w2w", tag="weight_words", align_bytes=64)
        nc.sync.dma_start(w2w[:].bitcast(I32), w2_words[0].bitcast(I32))
        w2s = keep.tile([P, N], U8, name="w2s", tag="weight_scales", align_bytes=64)
        nc.gpsimd.memset(w2s[:].bitcast(I32), 0)
        for q in range(QUADS):
            nc.sync.dma_start(
                w2s[32 * q : 32 * q + 4, :].bitcast(I32),
                w2_scales[0, 4 * q : 4 * q + 4, :].bitcast(I32),
            )
        dif = [sb(f"dif{t}", [P, S], F32) for t in range(PACK)]
        q_lag = [sb(f"q_lag{t}", [P, U], F32) for t in range(PACK)]
        poly = [sb(f"poly{h}", [P, PACK * RHALF], F32) for h in range(2)]

        def differences(t):
            for h in range(2):
                cols = slice(h * HALF, (h + 1) * HALF)
                nc.vector.tensor_tensor(
                    dif[t][:, cols], y_win[t][:].indirect(entries(shf_sb, h * HALF, HALF)), y_own[t][:, cols], ALU.subtract
                )

        def magnitudes(t, h):
            by_member = y_own[t][:, halves[h]].rearrange("p (d v) -> p v d", d=D)
            source = dif[t][:, halves[h]].rearrange("p (v d) -> p v d", d=D)
            if (t, h) in ABS_ON_VECTOR:
                nc.vector.scalar_tensor_tensor(by_member, source, -1.0, source, ALU.mult, ALU.max)
            else:
                nc.scalar.activation(by_member, source, ACT.Abs)
            turned = psum.tile([P, HALF], F32, name=f"bank{t}_{h}")
            for d in range(D):
                first = h * HALF + d * P
                nc.tensor.transpose(turned[:, d * P : (d + 1) * P], y_own[t][:, first : first + P], identity[:])
            return turned

        def roots(t):
            turned = [magnitudes(t, h) for h in range(2)]
            root = [keep.tile([P, HALF], F32, name=f"root{t}_{h}", tag=f"root{t}_{h}", align_bytes=64) for h in range(2)]
            nc.scalar.activation(root[0][:], turned[0][:], ACT.Sqrt, bias=0.05 / 16, scale=1.0 / 16)
            mean = psum.tile([P, HALF], F32, name=f"bank{t}_0")
            nc.scalar.activation(root[1][:], turned[1][:], ACT.Sqrt, bias=0.05 / 16, scale=1.0 / 16)
            for h in range(2):
                for d in range(D):
                    nc.tensor.matmul(
                        mean[:, h * P : (h + 1) * P],
                        root[h][:, d * P : (d + 1) * P],
                        identity[:],
                        start=(d == 0),
                        stop=(d == D - 1),
                        is_transpose=True,
                    )
            return mean

        def polynomial(t):
            looked = [q_lag[t][:, h * RHALF : (h + 1) * RHALF] for h in range(2)]
            mine = [poly[h][:, t * RHALF : (t + 1) * RHALF] for h in range(2)]
            for h in range(2):
                window = q_win[t][:].indirect(entries(lag_sb, h * RHALF, RHALF))
                if (t, h) in LAG_ON_VECTOR:
                    nc.vector.tensor_copy(looked[h], window)
                else:
                    nc.scalar.activation(looked[h], window, ACT.Copy)
            for h in range(2):
                first = t * U + h * RHALF
                nc.vector.tensor_tensor(mine[h], looked[h], lw_sb[:, first : first + RHALF], ALU.mult)
            for h in range(2):
                nc.vector.scalar_tensor_tensor(mine[h], mine[h], 0.1, looked[h], ALU.add, ALU.mult)

        rmean = []
        for t in range(PACK):
            differences(t)
            rmean.append(roots(t))
            nc.scalar.activation(q_win[t][:, :V], rmean[t][:, :V], ACT.Square)
        for t in range(PACK):
            polynomial(t)

        ln_z = keep.tile([P, PACK * V], F32, name="ln_z", tag=f"root{PACK - 1}_1", align_bytes=64)
        for t in range(PACK):
            mine = ln_z[:, t * V : (t + 1) * V]
            nc.scalar.activation(mine, q_win[t][:, :V], ACT.Ln, bias=0.6, scale=0.5)
            nc.vector.tensor_tensor(b_win[t][:, :V], rmean[t][:, :V], mine, ALU.subtract)

        ln_poly = [sb(f"ln_poly{h}", [P, PACK * RHALF], F32) for h in range(2)]
        total = [sb(f"total{h}", [P, PACK * RHALF], F32) for h in range(2)]
        hid = [sb(f"hid{h}", [P, RHALF * PACK], BF16) for h in range(2)]
        rounded = [sb(f"rounded{h}", [P, PACK * RHALF], BF16) for h in range(2)]

        def b_window(t, h):
            return b_win[t][:].indirect(entries(lag_sb, h * RHALF, RHALF))

        def scaled(h):
            for t in range(PACK):
                cols = slice(t * RHALF, (t + 1) * RHALF)
                if h in SCALE_ON_SCALAR:
                    nc.scalar.activation(rounded[h][:, cols], total[h][:, cols], ACT.Copy, scale=unit_sb[:, t : t + 1])
                else:
                    nc.vector.tensor_scalar(rounded[h][:, cols], total[h][:, cols], unit_sb[:, t : t + 1], None, ALU.mult)

        def woven(h, first, count):
            nc.vector.tensor_copy(
                hid[h][:, first * PACK : (first + count) * PACK].rearrange("p (c i t) -> p c t i", i=4, t=PACK),
                rounded[h][:].rearrange("p (t r) -> p t r", t=PACK)[:, :, first : first + count].rearrange(
                    "p t (c i) -> p c t i", i=4
                ),
            )

        def fitted(h, first, count, bank):
            codes = sb(f"codes{bank}", [P, count], U32)
            scales = sb(f"scales{bank}", [P, count], U8)
            nc.vector.quantize_mx(
                out=codes[:].bitcast(FP8X4), scales=scales[:], in_=hid[h][:, first * PACK : (first + count) * PACK]
            )
            fit = psum.tile([P, HALF], F32, name=f"bank{bank}_1")
            nc.tensor.matmul_mx(
                out=fit[:, :count],
                lhsT=w2w[:].bitcast(FP4X4),
                lhsT_scale=w2s[:],
                rhs=codes[:].bitcast(FP8X4),
                rhs_scale=scales[:],
                start=True,
                stop=True,
            )
            result = sb(f"result{bank}", [P, count], F32)
            nc.scalar.copy(result[:], fit[:, :count])
            column = h * RHALF + first
            nc.sync.dma_start(out[:, column : column + count], result[:])

        tiles = [slice(t * RHALF, (t + 1) * RHALF) for t in range(PACK)]
        b_lag = sb("b_lag", [P, PACK * RHALF], F32)
        nc.scalar.activation(ln_poly[0][:], poly[0][:], ACT.Ln, bias=0.12)
        for t in range(PACK):
            nc.vector.tensor_tensor(total[0][:, tiles[t]], b_window(t, 0), ln_poly[0][:, tiles[t]], ALU.add)
        nc.scalar.activation(ln_poly[1][:], poly[1][:], ACT.Ln, bias=0.12)
        for t in range(B_ON_SCALAR):
            nc.scalar.activation(b_lag[:, tiles[t]], b_window(t, 1), ACT.Copy)
        for t in range(B_ON_SCALAR, PACK):
            nc.vector.tensor_tensor(total[1][:, tiles[t]], b_window(t, 1), ln_poly[1][:, tiles[t]], ALU.add)
        scaled(0)
        fetched = slice(0, B_ON_SCALAR * RHALF)
        nc.vector.tensor_tensor(total[1][:, fetched], b_lag[:, fetched], ln_poly[1][:, fetched], ALU.add)
        woven(0, 0, RHALF)
        scaled(1)
        fitted(0, 0, RHALF, 0)
        quarter = RHALF // 2
        woven(1, 0, quarter)
        woven(1, quarter, quarter)
        fitted(1, 0, quarter, 1)
        fitted(1, quarter, quarter, 2)
